import numpy as np
import ml_dtypes


def mxq(x, axis, fmt="e4m3"):
    dtype, down = {"e4m3": (ml_dtypes.float8_e4m3fn, 7), "e5m2": (ml_dtypes.float8_e5m2, 14)}[fmt]
    v = np.moveaxis(np.asarray(x, np.float32).astype(ml_dtypes.bfloat16).astype(np.float64), axis, -1)
    blocks = v.reshape(v.shape[:-1] + (-1, 32))
    amax = np.abs(blocks).max(-1, keepdims=True)
    byte = np.maximum(np.where(amax > 0, np.frexp(amax)[1] - 1 + 127, 0) - down, 1)
    scale = np.exp2(byte - 127.0)
    codes = (blocks / scale).astype(np.float32).astype(dtype).astype(np.float64)
    return np.moveaxis((codes * scale).reshape(v.shape), -1, axis)


WIDE = False


def mx_kscale(k):
    if not WIDE:
        return np.ones(k)
    levels = np.array([10, -10, 5, -5, 0])
    if k % 512:
        return np.exp2(np.random.permutation(np.resize(levels, k // 32))).repeat(32)
    a = np.empty((k // 512, 16))
    for p in range(k // 512):
        a[p, :8] = np.random.permutation(np.resize(levels, 8))
        for g in range(8):
            far = levels[np.abs(levels - a[p, g]) >= 10]
            a[p, g + 8] = far[np.random.randint(len(far))]
    return np.exp2(a.ravel()).repeat(32)


def f64(x):
    return np.asarray(x).astype(np.float64)


def striped(idx):
    return np.tile(idx.reshape(-1, 16).T, (8, 1)).astype(np.uint16)


def unstriped(offs):
    return offs[:16].T.reshape(-1).astype(np.int64)


E2M1 = np.array([0.0, 0.5, 1.0, 1.5, 2.0, 3.0, 4.0, 6.0, -0.0, -0.5, -1.0, -1.5, -2.0, -3.0, -4.0, -6.0])


def pack_weight(w, fmt):
    k, n = w.shape
    w = f64(np.asarray(w, np.float32).astype(ml_dtypes.bfloat16)).reshape(k // 32, 32, n)
    amax = np.abs(w).max(1)
    if fmt == "e4m3":
        byte = np.frexp(amax)[1] - 1 + 127 - 7
    else:
        mant, ex = np.frexp(amax / 6.0)
        byte = np.where(mant > 0.5, ex, ex - 1) + 127
    byte = np.clip(np.where(amax > 0, byte, 1), 1, 254)
    scaled = (w * np.exp2(127.0 - byte)[:, None, :]).reshape(k, n).astype(np.float32)
    by_word = np.ascontiguousarray(scaled.reshape(k // 512, 128, 4, n).transpose(0, 1, 3, 2))
    if fmt == "e4m3":
        words = by_word.astype(ml_dtypes.float8_e4m3fn).view(np.uint8)
    else:
        c = by_word.astype(ml_dtypes.float4_e2m1fn).view(np.uint8) & 0xF
        words = (c[..., 0::2] | (c[..., 1::2] << 4)).reshape(k // 512, 128, 2 * n)
    return np.ascontiguousarray(words), np.ascontiguousarray(byte.astype(np.uint8).reshape(k // 512, 16, n))


def unpack_weight(words, scales, fmt):
    g, _, n = scales.shape
    words = np.ascontiguousarray(words).reshape(g, 128, n, -1)
    if fmt == "e4m3":
        vals = words.view(ml_dtypes.float8_e4m3fn).astype(np.float64)
    else:
        nib = np.empty((g, 128, n, 4), np.uint8)
        nib[..., 0::2] = words & 0xF
        nib[..., 1::2] = words >> 4
        vals = E2M1[nib]
    vals = vals * np.repeat(np.exp2(scales.astype(np.float64) - 127.0), 8, axis=1)[..., None]
    return vals.transpose(0, 1, 3, 2).reshape(g * 512, n)


def gelu(v):
    return 0.5 * v * (1.0 + np.tanh(np.sqrt(2.0 / np.pi) * (v + 0.044715 * v**3)))


K, H, T, S, T2, T3, S2 = 1024, 512, 4096, 1024, 2048, 2048, 512


def setup_inputs():
    n = np.random.standard_normal
    s = mx_kscale(K)[:, None]
    u = mx_kscale(H)[:, None]
    tab_words, tab_scales = pack_weight(n((K, T)) * s, "e4m3")
    tab2_words, tab2_scales = pack_weight(n((H, T3)) / np.sqrt(H) / u, "e4m3")
    w1_words, w1_scales = pack_weight(n((K, H)) / np.sqrt(K) / s * u.T, "e2m1")
    w3_words, w3_scales = pack_weight(n((K, H)) / np.sqrt(K) / s * u.T, "e4m3")
    return {
        "tab_words": tab_words, "tab_scales": tab_scales,
        "tab2_words": tab2_words, "tab2_scales": tab2_scales,
        "w1_words": w1_words, "w1_scales": w1_scales,
        "w2": (n((K, H)) / np.sqrt(K) / s * u.T).astype(np.float32),
        "w3_words": w3_words, "w3_scales": w3_scales,
        "cs": (0.9 * n(H)).astype(np.float32),
        "fl": (0.6 * n(S2)).astype(np.float32),
        "av": np.exp(0.4 * n(S2)).astype(np.float32),
        "page1": n((S2, T2)).astype(np.float32),
        "wgo": np.exp(0.3 * n((128, S))).astype(np.float32),
        "offs": striped(np.random.permutation(T)[:S]),
        "offs2": striped(np.random.permutation(T3)[:S2]),
        "offs3": striped(np.random.permutation(T2)[:S]),
    }


def reference(tab_words, tab_scales, tab2_words, tab2_scales, w1_words, w1_scales, w2,
              w3_words, w3_scales, cs, fl, av, page1, wgo, offs, offs2, offs3):
    v = unpack_weight(tab_words, tab_scales, "e4m3")[:, unstriped(offs)]
    v2 = unpack_weight(tab2_words, tab2_scales, "e4m3")[:, unstriped(offs2)]
    w1 = unpack_weight(w1_words, w1_scales, "e2m1")
    w3 = unpack_weight(w3_words, w3_scales, "e4m3")
    c1 = w1.T @ v
    c2 = mxq(f64(w2), 0, "e4m3").T @ v
    c3 = w3.T @ v
    h = f64(cs)[:, None] * c1 + np.maximum(c2, c3)
    e = v2.T @ mxq(h, 0, "e4m3")
    y = np.maximum(e, f64(fl)[:, None]) * f64(av)[:, None]
    out = f64(page1).copy()
    out[:, unstriped(offs3)] = np.tile(f64(wgo), (S2 // 128, 1)) * y
    return out

@@ -1,0 +1,255 @@
+from contextlib import ExitStack
+
+import concourse.mybir as mybir
+
+K, H, T, S, T2, T3, S2 = 1024, 512, 4096, 1024, 2048, 2048, 512
+FLOPS = 2 * 3 * K * H * S + 2 * H * S2 * S
+
+F32 = mybir.dt.float32
+BF16 = mybir.dt.bfloat16
+I32 = mybir.dt.int32
+U32 = mybir.dt.uint32
+U16 = mybir.dt.uint16
+U8 = mybir.dt.uint8
+FP8X4 = mybir.dt.float8_e4m3fn_x4
+FP4X4 = mybir.dt.float4_e2m1fn_x4
+MULT = mybir.AluOpType.mult
+ADD = mybir.AluOpType.add
+MAX = mybir.AluOpType.max
+
+P = 128
+PACK = 4
+PASSES = K // (P * PACK)
+QUADS = 4
+HALF = 512
+BANK = 512
+M_TILES = S2 // P
+CAST_SPLIT = 88
+
+
+def tile_list_chop_seeding_page_kernel(
+    tc, tab_words, tab_scales, tab2_words, tab2_scales, w1_words, w1_scales, w2,
+    w3_words, w3_scales, cs, fl, av, page1, wgo, offs, offs2, offs3, out,
+):
+    nc = tc.nc
+    with ExitStack() as ctx:
+        keep = ctx.enter_context(tc.tile_pool(name="keep", bufs=1))
+        ring = ctx.enter_context(tc.tile_pool(name="ring", bufs=2))
+        psum = ctx.enter_context(tc.psum_pool(name="psum", bufs=2))
+
+        def held(shape, dtype, name):
+            return keep.tile(shape, dtype, name=name, align_bytes=64)
+
+        idx = held([P, S // 16], U16, "idx")
+        idx2 = held([P, S2 // 16], U16, "idx2")
+        idx3 = held([P, S // 16], U16, "idx3")
+        tab = [held([P, T], I32, "tab%d" % a) for a in range(PASSES)]
+        tab_sc = held([P, T], U8, "tab_sc")
+        tab2 = held([P, T3], I32, "tab2")
+        tab2_sc = held([P, T3], U8, "tab2_sc")
+        w_sc_raw = held([P, PASSES * H], U8, "w_sc_raw")
+        w_sc = held([P, PASSES * H], U8, "w_sc")
+        w1_raw = held([P, PASSES * H * 2], U8, "w1_raw")
+        w1 = held([P, PASSES * H * 2], U8, "w1")
+        w3_raw = held([P, PASSES * H], I32, "w3_raw")
+        w3 = held([P, PASSES * H], I32, "w3")
+        w2_raw = [held([P, PACK * H], F32, "w2_raw%d" % a) for a in range(PASSES)]
+        w2_bf = [held([P, PACK * H], BF16, "w2_bf%d" % a) for a in range(PASSES)]
+        w2_q = [held([P, H], U32, "w2_q%d" % a) for a in range(PASSES)]
+        w2_sc = [held([P, H], U8, "w2_sc%d" % a) for a in range(PASSES)]
+        v = [[held([P, HALF], U32, "v%d_%d" % (a, u)) for u in range(S // HALF)] for a in range(PASSES)]
+        v_sc = held([P, S], U8, "v_sc")
+        v_sc1 = held([P, S], U8, "v_sc1")
+        v2 = held([P, S2], U32, "v2")
+        v2_sc = held([P, S2], U8, "v2_sc")
+        cs_sb = held([P, PACK], F32, "cs_sb")
+        fl_sb = held([P, M_TILES], F32, "fl_sb")
+        av_sb = held([P, M_TILES], F32, "av_sb")
+        wgo_sb = held([P, S], F32, "wgo_sb")
+        page = [held([P, T2], F32, "page%d" % m) for m in range(M_TILES)]
+
+        nc.vector.memset(w_sc_raw[:].bitcast(I32), 0)
+        nc.vector.memset(tab_sc[:].bitcast(I32), 0)
+        nc.vector.memset(tab2_sc[:].bitcast(I32), 0)
+        nc.vector.memset(v_sc1[:].bitcast(I32), 0)
+
+        def load_weight_scales(row0, scales):
+            for q in range(QUADS):
+                r = 32 * q + row0
+                nc.sync.dma_start(
+                    w_sc_raw[r : r + 4, :].bitcast(I32).rearrange("p (a c) -> p a c", a=PASSES),
+                    scales[:, 4 * q : 4 * q + 4, :].rearrange("a r c -> r a c").bitcast(I32),
+                )
+
+        nc.sync.dma_start(idx[:], offs)
+        nc.sync.dma_start(tab[0][:], tab_words[0].rearrange("p t i -> p (t i)").bitcast(I32))
+        nc.sync.dma_start(idx2[:], offs2)
+        load_weight_scales(4, w3_scales)
+        nc.sync.dma_start(tab[1][:], tab_words[1].rearrange("p t i -> p (t i)").bitcast(I32))
+        nc.sync.dma_start(
+            w3_raw[:].rearrange("p (a c) -> p a c", a=PASSES),
+            w3_words.rearrange("a p c i -> p a (c i)").bitcast(I32),
+        )
+        nc.sync.dma_start(
+            w1_raw[:].bitcast(I32).rearrange("p (a c) -> p a c", a=PASSES),
+            w1_words.rearrange("a p c -> p a c").bitcast(I32),
+        )
+        load_weight_scales(0, w1_scales)
+        for a in range(PASSES):
+            nc.sync.dma_start(
+                w2_raw[a][:], w2[512 * a : 512 * (a + 1), :].rearrange("(p j) c -> p (j c)", j=PACK)
+            )
+        nc.sync.dma_start(cs_sb[:], cs.rearrange("(p t) -> p t", t=PACK))
+        nc.sync.dma_start(tab2[:], tab2_words[0].rearrange("p t i -> p (t i)").bitcast(I32))
+        nc.sync.dma_start(idx3[:], offs3)
+        with nc.allow_non_contiguous_dma(reason="one value to a partition"):
+            nc.sync.dma_start(fl_sb[:], fl.rearrange("(m p) -> p m", p=P))
+            nc.sync.dma_start(av_sb[:], av.rearrange("(m p) -> p m", p=P))
+        nc.sync.dma_start(wgo_sb[:], wgo)
+        for m in range(M_TILES):
+            nc.sync.dma_start(page[m][:], page1[P * m : P * (m + 1), :])
+
+        for q in range(QUADS):
+            nc.gpsimd.dma_start(
+                tab_sc[32 * q : 32 * q + 8, :].bitcast(I32),
+                tab_scales[:, 4 * q : 4 * q + 4, :].bitcast(I32),
+            )
+
+        nc.vector.tensor_copy(v_sc[:], tab_sc[:].indirect(idx[:]))
+        for q in range(QUADS):
+            nc.gpsimd.dma_start(
+                v_sc1[32 * q : 32 * q + 4, :].bitcast(I32), v_sc[32 * q + 4 : 32 * q + 8, :].bitcast(I32)
+            )
+        for q in range(QUADS):
+            nc.gpsimd.dma_start(
+                tab2_sc[32 * q : 32 * q + 4, :].bitcast(I32),
+                tab2_scales[0, 4 * q : 4 * q + 4, :].bitcast(I32),
+            )
+        for a in range(PASSES):
+            for u in range(S // HALF):
+                cols = slice(u * HALF // 16, (u + 1) * HALF // 16)
+                nc.vector.tensor_copy(v[a][u][:], tab[a][:].bitcast(U32).indirect(idx[:, cols]))
+
+        nc.vector.tensor_copy(
+            w_sc[:].rearrange("p (a t q) -> p a q t", a=PASSES, t=PACK),
+            w_sc_raw[:].rearrange("p (a q t) -> p a q t", a=PASSES, t=PACK),
+        )
+        nc.vector.tensor_copy(
+            w3[:].rearrange("p (a t q) -> p a q t", a=PASSES, t=PACK),
+            w3_raw[:].rearrange("p (a q t) -> p a q t", a=PASSES, t=PACK),
+        )
+        nc.vector.tensor_copy(
+            w1[:].bitcast(U16).rearrange("p (a t q) -> p a q t", a=PASSES, t=PACK),
+            w1_raw[:].bitcast(U16).rearrange("p (a q t) -> p a q t", a=PASSES, t=PACK),
+        )
+        for a in range(PASSES):
+            dst = w2_bf[a][:].rearrange("p (t q j) -> p q j t", t=PACK, j=PACK)
+            src = w2_raw[a][:].rearrange("p (j q t) -> p q j t", t=PACK, j=PACK)
+            nc.scalar.copy(dst[:, CAST_SPLIT:], src[:, CAST_SPLIT:])
+            nc.vector.tensor_copy(dst[:, :CAST_SPLIT], src[:, :CAST_SPLIT])
+            for u in range(2):
+                nc.vector.quantize_mx(
+                    out=w2_q[a][:, 256 * u : 256 * (u + 1)].bitcast(FP8X4),
+                    scales=w2_sc[a][:, 256 * u : 256 * (u + 1)],
+                    in_=w2_bf[a][:, 1024 * u : 1024 * (u + 1)],
+                )
+
+        nc.vector.tensor_copy(v2_sc[:], tab2_sc[:].indirect(idx2[:]))
+        nc.vector.tensor_copy(v2[:], tab2[:].bitcast(U32).indirect(idx2[:]))
+
+        def moving(a, tok):
+            u, o = divmod(tok.start, HALF)
+            return v[a][u][:, o : o + tok.stop - tok.start].bitcast(FP8X4)
+
+        def features(tok, last_larger_tag, h_bf_tag):
+            width = tok.stop - tok.start
+            per_bank = BANK // width
+            h_planes = ring.tile([P, PACK, width], BF16, name="h_planes", align_bytes=64)
+            for t0 in range(0, PACK, per_bank):
+                c1 = psum.tile([P, per_bank, width], F32, name="c1")
+                c2 = psum.tile([P, per_bank, width], F32, name="c2")
+                c3 = psum.tile([P, per_bank, width], F32, name="c3")
+                for i in range(per_bank):
+                    t = t0 + i
+                    for a in range(PASSES):
+                        w = slice(a * H + t * P, a * H + (t + 1) * P)
+                        nc.tensor.matmul_mx(
+                            out=c3[:, i, :], lhsT=w3[:, w].bitcast(FP8X4), lhsT_scale=w_sc[4:P, w],
+                            rhs=moving(a, tok), rhs_scale=v_sc[4 * a : P, tok],
+                            start=(a == 0), stop=(a == PASSES - 1),
+                        )
+                for a in range(PASSES):
+                    for i in range(per_bank):
+                        t = t0 + i
+                        w = slice(t * P, (t + 1) * P)
+                        nc.tensor.matmul_mx(
+                            out=c2[:, i, :], lhsT=w2_q[a][:, w].bitcast(FP8X4), lhsT_scale=w2_sc[a][:, w],
+                            rhs=moving(a, tok), rhs_scale=v_sc[4 * a : P, tok],
+                            start=(a == 0 and i == 0), stop=(a == PASSES - 1 and i == per_bank - 1),
+                        )
+                for i in range(per_bank):
+                    t = t0 + i
+                    for a in range(PASSES):
+                        w0 = a * H + t * P
+                        nc.tensor.matmul_mx(
+                            out=c1[:, i, :], lhsT=w1[:, 2 * w0 : 2 * (w0 + P)].bitcast(FP4X4),
+                            lhsT_scale=w_sc[:, w0 : w0 + P],
+                            rhs=moving(a, tok), rhs_scale=(v_sc, v_sc1)[a][:, tok],
+                            start=(a == 0), stop=(a == PASSES - 1),
+                        )
+                c3_sb = ring.tile([P, per_bank, width], F32, name="c3_sb")
+                nc.scalar.copy(c3_sb[:], c3[:])
+                if t0 + per_bank == PACK and last_larger_tag:
+                    larger = keep.tile([P, per_bank, width], F32, name="larger_last", tag=last_larger_tag, align_bytes=64)
+                else:
+                    larger = ring.tile([P, per_bank, width], F32, name="larger")
+                nc.vector.tensor_tensor(larger[:], c2[:], c3_sb[:], MAX)
+                for i in range(per_bank):
+                    t = t0 + i
+                    nc.vector.scalar_tensor_tensor(
+                        h_planes[:, t, :], c1[:, i, :], cs_sb[:, t : t + 1], larger[:, i, :], MULT, ADD
+                    )
+            h_bf = keep.tile([P, width * PACK], BF16, name="h_bf", tag=h_bf_tag, align_bytes=64)
+            nc.scalar.copy(
+                h_bf[:].rearrange("p (c i t) -> p c t i", i=4, t=PACK),
+                h_planes[:].rearrange("p t (c i) -> p c t i", i=4),
+            )
+            h_q = ring.tile([P, width], U32, name="h_q", align_bytes=64)
+            h_sc = ring.tile([P, width], U8, name="h_sc", align_bytes=64)
+            nc.vector.quantize_mx(out=h_q[:].bitcast(FP8X4), scales=h_sc[:], in_=h_bf[:])
+            return h_q, h_sc
+
+        def scores(tok, h_q, h_sc, y_tags, last):
+            width = tok.stop - tok.start
+            per_bank = BANK // width
+            cols = slice(tok.start // 16, tok.stop // 16)
+            for g, m0 in enumerate(range(0, M_TILES, per_bank)):
+                e = psum.tile([P, per_bank, width], F32, name="e")
+                for i in range(per_bank):
+                    m = m0 + i
+                    nc.tensor.matmul_mx(
+                        out=e[:, i, :], lhsT=v2[:, m * P : (m + 1) * P].bitcast(FP8X4),
+                        lhsT_scale=v2_sc[:, m * P : (m + 1) * P],
+                        rhs=h_q[:].bitcast(FP8X4), rhs_scale=h_sc[:], start=True, stop=True,
+                    )
+                e_sb = ring.tile([P, per_bank, width], F32, name="e_sb", bufs=4)
+                nc.scalar.copy(e_sb[:], e[:])
+                y = keep.tile([P, per_bank, width], F32, name="y", tag=y_tags[g], align_bytes=64)
+                for i in range(per_bank):
+                    m = m0 + i
+                    nc.vector.tensor_scalar(
+                        y[:, i, :], e_sb[:, i, :], fl_sb[:, m : m + 1], av_sb[:, m : m + 1], MAX, MULT
+                    )
+                for i in range(per_bank):
+                    m = m0 + i
+                    nc.vector.tensor_tensor(page[m][:].indirect(idx3[:, cols]), y[:, i, :], wgo_sb[:, tok], MULT)
+                    if last:
+                        nc.sync.dma_start(out[P * m : P * (m + 1), :], page[m][:])
+
+        first, second, third = slice(0, 256), slice(256, 512), slice(512, 1024)
+        h0 = features(first, None, "h_bf0")
+        h1 = features(second, None, "h_bf1")
+        scores(first, *h0, ("y0a", "y0b"), False)
+        h2 = features(third, "hold_a", "hold_b")
+        scores(second, *h1, ("hold_a", "hold_b"), False)
+        scores(third, *h2, ("y2a", "y2b", "y2c", "y2d"), True)

@@ -24,7 +24,7 @@ QUADS = 4
 HALF = 512
 BANK = 512
 M_TILES = S2 // P
-CAST_SPLIT = 88
+CAST_SPLIT = (88, 48)
 
 
 def tile_list_chop_seeding_page_kernel(
@@ -58,8 +58,8 @@ def tile_list_chop_seeding_page_kernel(
         w2_q = [held([P, H], U32, "w2_q%d" % a) for a in range(PASSES)]
         w2_sc = [held([P, H], U8, "w2_sc%d" % a) for a in range(PASSES)]
         v = [[held([P, HALF], U32, "v%d_%d" % (a, u)) for u in range(S // HALF)] for a in range(PASSES)]
-        v_sc = held([P, S], U8, "v_sc")
-        v_sc1 = held([P, S], U8, "v_sc1")
+        v_sc_rows = held([P, S], U8, "v_sc_rows")
+        v_sc = [held([P, S], U8, "v_sc%d" % a) for a in range(PASSES)]
         v2 = held([P, S2], U32, "v2")
         v2_sc = held([P, S2], U8, "v2_sc")
         cs_sb = held([P, PACK], F32, "cs_sb")
@@ -69,39 +69,69 @@ def tile_list_chop_seeding_page_kernel(
         page = [held([P, T2], F32, "page%d" % m) for m in range(M_TILES)]
 
         nc.vector.memset(w_sc_raw[:].bitcast(I32), 0)
-        nc.vector.memset(tab_sc[:].bitcast(I32), 0)
-        nc.vector.memset(tab2_sc[:].bitcast(I32), 0)
-        nc.vector.memset(v_sc1[:].bitcast(I32), 0)
+        nc.vector.memset(tab_sc[32:64, :].bitcast(I32), 0)
+        nc.vector.memset(tab_sc[64:128, :].bitcast(I32), 0)
+        for a in range(PASSES):
+            nc.vector.memset(v_sc[a][:].bitcast(I32), 0)
+        nc.gpsimd.memset(tab2_sc[:].bitcast(I32), 0)
 
-        def load_weight_scales(row0, scales):
-            for q in range(QUADS):
-                r = 32 * q + row0
-                nc.sync.dma_start(
-                    w_sc_raw[r : r + 4, :].bitcast(I32).rearrange("p (a c) -> p a c", a=PASSES),
-                    scales[:, 4 * q : 4 * q + 4, :].rearrange("a r c -> r a c").bitcast(I32),
-                )
+        def load_weight_scales(row0, scales, q):
+            r = 32 * q + row0
+            nc.sync.dma_start(
+                w_sc_raw[r : r + 4, :].bitcast(I32).rearrange("p (a c) -> p a c", a=PASSES),
+                scales[:, 4 * q : 4 * q + 4, :].rearrange("a r c -> r a c").bitcast(I32),
+            )
 
+        def load_table_half(a, u):
+            cols = slice(u * T // 2, (u + 1) * T // 2)
+            nc.sync.dma_start(tab[a][:, cols], tab_words[a].rearrange("p t i -> p (t i)").bitcast(I32)[:, cols])
+
+        def move_plane(a, q):
+            r = 16 * a + 4 * q
+            nc.sync.dma_start(v_sc[a][32 * q : 32 * q + 4, :].bitcast(I32), v_sc_rows[r : r + 4, :].bitcast(I32))
+
+        def load_w2(a):
+            nc.sync.dma_start(
+                w2_raw[a][:], w2[512 * a : 512 * (a + 1), :].rearrange("(p j) c -> p (j c)", j=PACK)
+            )
+
+        nc.sync.dma_start(tab_sc[0:32, :].bitcast(I32), tab_scales.rearrange("a q t -> (a q) t").bitcast(I32))
         nc.sync.dma_start(idx[:], offs)
-        nc.sync.dma_start(tab[0][:], tab_words[0].rearrange("p t i -> p (t i)").bitcast(I32))
+        load_table_half(0, 0)
         nc.sync.dma_start(idx2[:], offs2)
-        load_weight_scales(4, w3_scales)
-        nc.sync.dma_start(tab[1][:], tab_words[1].rearrange("p t i -> p (t i)").bitcast(I32))
+        nc.sync.dma_start(idx3[:], offs3)
+        nc.sync.dma_start(cs_sb[:], cs.rearrange("(p t) -> p t", t=PACK))
+        load_table_half(0, 1)
         nc.sync.dma_start(
             w3_raw[:].rearrange("p (a c) -> p a c", a=PASSES),
             w3_words.rearrange("a p c i -> p a (c i)").bitcast(I32),
         )
+        load_weight_scales(4, w3_scales, 0)
+        load_weight_scales(4, w3_scales, 1)
         nc.sync.dma_start(
             w1_raw[:].bitcast(I32).rearrange("p (a c) -> p a c", a=PASSES),
             w1_words.rearrange("a p c -> p a c").bitcast(I32),
         )
-        load_weight_scales(0, w1_scales)
-        for a in range(PASSES):
+        load_weight_scales(4, w3_scales, 2)
+        load_weight_scales(4, w3_scales, 3)
+        load_table_half(1, 0)
+        for q in range(QUADS):
+            load_weight_scales(0, w1_scales, q)
+        nc.vector.tensor_copy(v_sc_rows[:], tab_sc[:].indirect(idx[:]))
+        moves = [(a, q) for a in range(PASSES) for q in range(QUADS)]
+        for a, q in moves[:2]:
+            move_plane(a, q)
+        load_table_half(1, 1)
+        for a, q in moves[2:]:
+            move_plane(a, q)
+        load_w2(0)
+        for q in range(QUADS):
             nc.sync.dma_start(
-                w2_raw[a][:], w2[512 * a : 512 * (a + 1), :].rearrange("(p j) c -> p (j c)", j=PACK)
+                tab2_sc[32 * q : 32 * q + 4, :].bitcast(I32),
+                tab2_scales[0, 4 * q : 4 * q + 4, :].bitcast(I32),
             )
-        nc.sync.dma_start(cs_sb[:], cs.rearrange("(p t) -> p t", t=PACK))
+        load_w2(1)
         nc.sync.dma_start(tab2[:], tab2_words[0].rearrange("p t i -> p (t i)").bitcast(I32))
-        nc.sync.dma_start(idx3[:], offs3)
         with nc.allow_non_contiguous_dma(reason="one value to a partition"):
             nc.sync.dma_start(fl_sb[:], fl.rearrange("(m p) -> p m", p=P))
             nc.sync.dma_start(av_sb[:], av.rearrange("(m p) -> p m", p=P))
@@ -109,31 +139,13 @@ def tile_list_chop_seeding_page_kernel(
         for m in range(M_TILES):
             nc.sync.dma_start(page[m][:], page1[P * m : P * (m + 1), :])
 
-        for q in range(QUADS):
-            nc.gpsimd.dma_start(
-                tab_sc[32 * q : 32 * q + 8, :].bitcast(I32),
-                tab_scales[:, 4 * q : 4 * q + 4, :].bitcast(I32),
-            )
-
-        nc.vector.tensor_copy(v_sc[:], tab_sc[:].indirect(idx[:]))
-        for q in range(QUADS):
-            nc.gpsimd.dma_start(
-                v_sc1[32 * q : 32 * q + 4, :].bitcast(I32), v_sc[32 * q + 4 : 32 * q + 8, :].bitcast(I32)
-            )
-        for q in range(QUADS):
-            nc.gpsimd.dma_start(
-                tab2_sc[32 * q : 32 * q + 4, :].bitcast(I32),
-                tab2_scales[0, 4 * q : 4 * q + 4, :].bitcast(I32),
-            )
-        for a in range(PASSES):
+        def gather_table(a):
             for u in range(S // HALF):
                 cols = slice(u * HALF // 16, (u + 1) * HALF // 16)
                 nc.vector.tensor_copy(v[a][u][:], tab[a][:].bitcast(U32).indirect(idx[:, cols]))
 
-        nc.vector.tensor_copy(
-            w_sc[:].rearrange("p (a t q) -> p a q t", a=PASSES, t=PACK),
-            w_sc_raw[:].rearrange("p (a q t) -> p a q t", a=PASSES, t=PACK),
-        )
+        gather_table(0)
+
         nc.vector.tensor_copy(
             w3[:].rearrange("p (a t q) -> p a q t", a=PASSES, t=PACK),
             w3_raw[:].rearrange("p (a q t) -> p a q t", a=PASSES, t=PACK),
@@ -142,11 +154,18 @@ def tile_list_chop_seeding_page_kernel(
             w1[:].bitcast(U16).rearrange("p (a t q) -> p a q t", a=PASSES, t=PACK),
             w1_raw[:].bitcast(U16).rearrange("p (a q t) -> p a q t", a=PASSES, t=PACK),
         )
+        nc.vector.tensor_copy(
+            w_sc[:].rearrange("p (a t q) -> p a q t", a=PASSES, t=PACK),
+            w_sc_raw[:].rearrange("p (a q t) -> p a q t", a=PASSES, t=PACK),
+        )
+        gather_table(1)
         for a in range(PASSES):
             dst = w2_bf[a][:].rearrange("p (t q j) -> p q j t", t=PACK, j=PACK)
             src = w2_raw[a][:].rearrange("p (j q t) -> p q j t", t=PACK, j=PACK)
-            nc.scalar.copy(dst[:, CAST_SPLIT:], src[:, CAST_SPLIT:])
-            nc.vector.tensor_copy(dst[:, :CAST_SPLIT], src[:, :CAST_SPLIT])
+            for u in range(2):
+                split, ts = CAST_SPLIT[u], slice(2 * u, 2 * u + 2)
+                nc.scalar.copy(dst[:, split:, :, ts], src[:, split:, :, ts])
+                nc.vector.tensor_copy(dst[:, :split, :, ts], src[:, :split, :, ts])
             for u in range(2):
                 nc.vector.quantize_mx(
                     out=w2_q[a][:, 256 * u : 256 * (u + 1)].bitcast(FP8X4),
@@ -175,7 +194,7 @@ def tile_list_chop_seeding_page_kernel(
                         w = slice(a * H + t * P, a * H + (t + 1) * P)
                         nc.tensor.matmul_mx(
                             out=c3[:, i, :], lhsT=w3[:, w].bitcast(FP8X4), lhsT_scale=w_sc[4:P, w],
-                            rhs=moving(a, tok), rhs_scale=v_sc[4 * a : P, tok],
+                            rhs=moving(a, tok), rhs_scale=v_sc[a][:, tok],
                             start=(a == 0), stop=(a == PASSES - 1),
                         )
                 for a in range(PASSES):
@@ -184,7 +203,7 @@ def tile_list_chop_seeding_page_kernel(
                         w = slice(t * P, (t + 1) * P)
                         nc.tensor.matmul_mx(
                             out=c2[:, i, :], lhsT=w2_q[a][:, w].bitcast(FP8X4), lhsT_scale=w2_sc[a][:, w],
-                            rhs=moving(a, tok), rhs_scale=v_sc[4 * a : P, tok],
+                            rhs=moving(a, tok), rhs_scale=v_sc[a][:, tok],
                             start=(a == 0 and i == 0), stop=(a == PASSES - 1 and i == per_bank - 1),
                         )
                 for i in range(per_bank):
@@ -194,7 +213,7 @@ def tile_list_chop_seeding_page_kernel(
                         nc.tensor.matmul_mx(
                             out=c1[:, i, :], lhsT=w1[:, 2 * w0 : 2 * (w0 + P)].bitcast(FP4X4),
                             lhsT_scale=w_sc[:, w0 : w0 + P],
-                            rhs=moving(a, tok), rhs_scale=(v_sc, v_sc1)[a][:, tok],
+                            rhs=moving(a, tok), rhs_scale=v_sc[a][:, tok],
                             start=(a == 0), stop=(a == PASSES - 1),
                         )
                 c3_sb = ring.tile([P, per_bank, width], F32, name="c3_sb")

@@ -1,6 +1,7 @@
 from contextlib import ExitStack
 
 import concourse.mybir as mybir
+from concourse.masks import make_identity
 
 K, H, T, S, T2, T3, S2 = 1024, 512, 4096, 1024, 2048, 2048, 512
 FLOPS = 2 * 3 * K * H * S + 2 * H * S2 * S
@@ -16,6 +17,7 @@ FP4X4 = mybir.dt.float4_e2m1fn_x4
 MULT = mybir.AluOpType.mult
 ADD = mybir.AluOpType.add
 MAX = mybir.AluOpType.max
+COPY = mybir.ActivationFunctionType.Copy
 
 P = 128
 PACK = 4
@@ -67,6 +69,9 @@ def tile_list_chop_seeding_page_kernel(
         av_sb = held([P, M_TILES], F32, "av_sb")
         wgo_sb = held([P, S], F32, "wgo_sb")
         page = [held([P, T2], F32, "page%d" % m) for m in range(M_TILES)]
+
+        ident = held([P, P], F32, "ident")
+        make_identity(nc, ident[:])
 
         nc.vector.memset(w_sc_raw[:].bitcast(I32), 0)
         nc.vector.memset(tab_sc[32:64, :].bitcast(I32), 0)
@@ -180,69 +185,117 @@ def tile_list_chop_seeding_page_kernel(
             u, o = divmod(tok.start, HALF)
             return v[a][u][:, o : o + tok.stop - tok.start].bitcast(FP8X4)
 
-        def features(tok, last_larger_tag, h_bf_tag):
+        def products(tok, t0, per_bank):
             width = tok.stop - tok.start
-            per_bank = BANK // width
-            h_planes = ring.tile([P, PACK, width], BF16, name="h_planes", align_bytes=64)
-            for t0 in range(0, PACK, per_bank):
-                c1 = psum.tile([P, per_bank, width], F32, name="c1")
-                c2 = psum.tile([P, per_bank, width], F32, name="c2")
-                c3 = psum.tile([P, per_bank, width], F32, name="c3")
-                for i in range(per_bank):
-                    t = t0 + i
-                    for a in range(PASSES):
-                        w = slice(a * H + t * P, a * H + (t + 1) * P)
-                        nc.tensor.matmul_mx(
-                            out=c3[:, i, :], lhsT=w3[:, w].bitcast(FP8X4), lhsT_scale=w_sc[4:P, w],
-                            rhs=moving(a, tok), rhs_scale=v_sc[a][:, tok],
-                            start=(a == 0), stop=(a == PASSES - 1),
-                        )
+            c1 = psum.tile([P, per_bank, width], F32, name="c1")
+            c2 = psum.tile([P, per_bank, width], F32, name="c2")
+            c3 = psum.tile([P, per_bank, width], F32, name="c3")
+            for i in range(per_bank):
+                t = t0 + i
                 for a in range(PASSES):
-                    for i in range(per_bank):
-                        t = t0 + i
-                        w = slice(t * P, (t + 1) * P)
-                        nc.tensor.matmul_mx(
-                            out=c2[:, i, :], lhsT=w2_q[a][:, w].bitcast(FP8X4), lhsT_scale=w2_sc[a][:, w],
-                            rhs=moving(a, tok), rhs_scale=v_sc[a][:, tok],
-                            start=(a == 0 and i == 0), stop=(a == PASSES - 1 and i == per_bank - 1),
-                        )
-                for i in range(per_bank):
-                    t = t0 + i
-                    for a in range(PASSES):
-                        w0 = a * H + t * P
-                        nc.tensor.matmul_mx(
-                            out=c1[:, i, :], lhsT=w1[:, 2 * w0 : 2 * (w0 + P)].bitcast(FP4X4),
-                            lhsT_scale=w_sc[:, w0 : w0 + P],
-                            rhs=moving(a, tok), rhs_scale=v_sc[a][:, tok],
-                            start=(a == 0), stop=(a == PASSES - 1),
-                        )
-                c3_sb = ring.tile([P, per_bank, width], F32, name="c3_sb")
-                nc.scalar.copy(c3_sb[:], c3[:])
-                if t0 + per_bank == PACK and last_larger_tag:
-                    larger = keep.tile([P, per_bank, width], F32, name="larger_last", tag=last_larger_tag, align_bytes=64)
-                else:
-                    larger = ring.tile([P, per_bank, width], F32, name="larger")
-                nc.vector.tensor_tensor(larger[:], c2[:], c3_sb[:], MAX)
-                for i in range(per_bank):
-                    t = t0 + i
-                    nc.vector.scalar_tensor_tensor(
-                        h_planes[:, t, :], c1[:, i, :], cs_sb[:, t : t + 1], larger[:, i, :], MULT, ADD
+                    w = slice(a * H + t * P, a * H + (t + 1) * P)
+                    nc.tensor.matmul_mx(
+                        out=c3[:, i, :], lhsT=w3[:, w].bitcast(FP8X4), lhsT_scale=w_sc[4:P, w],
+                        rhs=moving(a, tok), rhs_scale=v_sc[a][:, tok],
+                        start=(a == 0), stop=(a == PASSES - 1),
                     )
-            h_bf = keep.tile([P, width * PACK], BF16, name="h_bf", tag=h_bf_tag, align_bytes=64)
-            nc.scalar.copy(
-                h_bf[:].rearrange("p (c i t) -> p c t i", i=4, t=PACK),
-                h_planes[:].rearrange("p t (c i) -> p c t i", i=4),
-            )
+            for a in range(PASSES):
+                for i in range(per_bank):
+                    t = t0 + i
+                    w = slice(t * P, (t + 1) * P)
+                    nc.tensor.matmul_mx(
+                        out=c2[:, i, :], lhsT=w2_q[a][:, w].bitcast(FP8X4), lhsT_scale=w2_sc[a][:, w],
+                        rhs=moving(a, tok), rhs_scale=v_sc[a][:, tok],
+                        start=(a == 0 and i == 0), stop=(a == PASSES - 1 and i == per_bank - 1),
+                    )
+            for i in range(per_bank):
+                t = t0 + i
+                for a in range(PASSES):
+                    w0 = a * H + t * P
+                    nc.tensor.matmul_mx(
+                        out=c1[:, i, :], lhsT=w1[:, 2 * w0 : 2 * (w0 + P)].bitcast(FP4X4),
+                        lhsT_scale=w_sc[:, w0 : w0 + P],
+                        rhs=moving(a, tok), rhs_scale=v_sc[a][:, tok],
+                        start=(a == 0), stop=(a == PASSES - 1),
+                    )
+            return c1, c2, c3
+
+        def quantise_h(h_bf, width):
             h_q = ring.tile([P, width], U32, name="h_q", align_bytes=64)
             h_sc = ring.tile([P, width], U8, name="h_sc", align_bytes=64)
             nc.vector.quantize_mx(out=h_q[:].bitcast(FP8X4), scales=h_sc[:], in_=h_bf[:])
             return h_q, h_sc
 
-        def scores(tok, h_q, h_sc, y_tags, last):
+        def features(tok):
             width = tok.stop - tok.start
             per_bank = BANK // width
-            cols = slice(tok.start // 16, tok.stop // 16)
-            for g, m0 in enumerate(range(0, M_TILES, per_bank)):
+            h_planes = ring.tile([P, PACK, width], BF16, name="h_planes", align_bytes=64)
+            banks = []
+            for t0 in range(0, PACK, per_bank):
+                c1, c2, c3 = products(tok, t0, per_bank)
+                c3_sb = ring.tile([P, per_bank, width], F32, name="c3_sb")
+                nc.scalar.copy(c3_sb[:], c3[:])
+                larger = ring.tile([P, per_bank, width], F32, name="larger")
+                nc.vector.tensor_tensor(larger[:], c2[:], c3_sb[:], MAX)
+                banks.append((t0, c1, larger))
+            for t0, c1, larger in banks:
+                for i in range(per_bank):
+                    t = t0 + i
+                    nc.vector.scalar_tensor_tensor(
+                        h_planes[:, t, :], c1[:, i, :], cs_sb[:, t : t + 1], larger[:, i, :], MULT, ADD
+                    )
+            h_bf = ring.tile([P, width * PACK], BF16, name="h_bf", align_bytes=64)
+            nc.scalar.copy(
+                h_bf[:].rearrange("p (c i t) -> p c t i", i=4, t=PACK),
+                h_planes[:].rearrange("p t (c i) -> p c t i", i=4),
+            )
+            return quantise_h(h_bf, width)
+
+        def features_added_in_psum(tok):
+            blocks = BANK // P
+            terms = []
+            for t in range(PACK):
+                c1, c2, c3 = products(tok, t, 1)
+                if t == PACK - 1:
+                    c3_sb = keep.tile([P, BANK], F32, name="c3_last", tag="hold_a", align_bytes=64)
+                else:
+                    c3_sb = ring.tile([P, BANK], F32, name="c3_sb")
+                nc.scalar.copy(c3_sb[:], c3[:, 0, :])
+                scaled = held([P, BANK], F32, "scaled%d" % t)
+                nc.scalar.activation(scaled[:], c1[:, 0, :], COPY, scale=cs_sb[:, t : t + 1])
+                larger = held([P, BANK], F32, "larger%d" % t)
+                nc.vector.tensor_tensor(larger[:], c2[:, 0, :], c3_sb[:], MAX)
+                terms.append((scaled, larger))
+            h_bf = keep.tile([P, BANK * PACK], BF16, name="h_bf_last", tag="hold_b", align_bytes=64)
+            sums = [psum.tile([P, PACK, P], F32, name="h_t", tag=tag) for tag in ("e", "e", "c1", "c3")]
+            for t in range(PACK):
+                for b in range(blocks):
+                    for n, term in enumerate(terms[t]):
+                        nc.tensor.matmul(
+                            sums[b][:, t, :], term[:, b * P : (b + 1) * P], ident[:],
+                            start=(n == 0), stop=(n == 1), is_transpose=True,
+                        )
+            for b0 in range(0, blocks, 2):
+                words = psum.tile([P, 2, 2, P], F32, name="words", tag="c2")
+                for i in range(2):
+                    h_t = ring.tile([P, 2 * P * 2], BF16, name="h_t_bf", bufs=4, align_bytes=64)
+                    nc.scalar.copy(
+                        h_t[:].rearrange("p (u q e) -> p u q e", u=2, e=2),
+                        sums[b0 + i][:].rearrange("p (u e) q -> p u q e", u=2),
+                    )
+                    for u in range(2):
+                        nc.tensor.transpose(words[:, i, u, :], h_t[:].bitcast(F32)[:, u * P : (u + 1) * P], ident[:])
+                nc.scalar.copy(
+                    h_bf[:].bitcast(F32)[:, b0 * 2 * P : (b0 + 2) * 2 * P].rearrange("p (b n u) -> p b n u", b=2, u=2),
+                    words[:].rearrange("p b u n -> p b n u"),
+                )
+            return quantise_h(h_bf, BANK)
+
+        def scores(tok, h_q, h_sc):
+            width = tok.stop - tok.start
+            per_bank = BANK // width
+            rows = []
+            for m0 in range(0, M_TILES, per_bank):
                 e = psum.tile([P, per_bank, width], F32, name="e")
                 for i in range(per_bank):
                     m = m0 + i
@@ -253,22 +306,28 @@ def tile_list_chop_seeding_page_kernel(
                     )
                 e_sb = ring.tile([P, per_bank, width], F32, name="e_sb", bufs=4)
                 nc.scalar.copy(e_sb[:], e[:])
-                y = keep.tile([P, per_bank, width], F32, name="y", tag=y_tags[g], align_bytes=64)
-                for i in range(per_bank):
-                    m = m0 + i
+                rows.extend([e_sb[:, i, :] for i in range(per_bank)])
+            return rows
+
+        def place(tok, e_rows, groups, last):
+            width = tok.stop - tok.start
+            cols = slice(tok.start // 16, tok.stop // 16)
+            for tag, ms in groups:
+                y = keep.tile([P, len(ms), width], F32, name="y", tag=tag, align_bytes=64)
+                for i, m in enumerate(ms):
                     nc.vector.tensor_scalar(
-                        y[:, i, :], e_sb[:, i, :], fl_sb[:, m : m + 1], av_sb[:, m : m + 1], MAX, MULT
+                        y[:, i, :], e_rows[m], fl_sb[:, m : m + 1], av_sb[:, m : m + 1], MAX, MULT
                     )
-                for i in range(per_bank):
-                    m = m0 + i
+                for i, m in enumerate(ms):
                     nc.vector.tensor_tensor(page[m][:].indirect(idx3[:, cols]), y[:, i, :], wgo_sb[:, tok], MULT)
                     if last:
                         nc.sync.dma_start(out[P * m : P * (m + 1), :], page[m][:])
 
         first, second, third = slice(0, 256), slice(256, 512), slice(512, 1024)
-        h0 = features(first, None, "h_bf0")
-        h1 = features(second, None, "h_bf1")
-        scores(first, *h0, ("y0a", "y0b"), False)
-        h2 = features(third, "hold_a", "hold_b")
-        scores(second, *h1, ("hold_a", "hold_b"), False)
-        scores(third, *h2, ("y2a", "y2b", "y2c", "y2d"), True)
+        h0 = features(first)
+        h1 = features(second)
+        place(first, scores(first, *h0), (("y0a", (0, 1)), ("y0b", (2, 3))), False)
+        e1 = scores(second, *h1)
+        h2 = features_added_in_psum(third)
+        place(second, e1, (("hold_a", (0, 1)), ("hold_b", (2, 3))), False)
+        place(third, scores(third, *h2), (("y2a", (0,)), ("y2b", (1,)), ("y2c", (2,)), ("y2d", (3,))), True)

@@ -1,4 +1,5 @@
 from contextlib import ExitStack
+from functools import partial
 
 import concourse.mybir as mybir
 from concourse.masks import make_identity
@@ -27,6 +28,7 @@ HALF = 512
 BANK = 512
 M_TILES = S2 // P
 CAST_SPLIT = (88, 48)
+SMALL_RUN = 6
 
 
 def tile_list_chop_seeding_page_kernel(
@@ -63,6 +65,7 @@ def tile_list_chop_seeding_page_kernel(
         v_sc_rows = held([P, S], U8, "v_sc_rows")
         v_sc = [held([P, S], U8, "v_sc%d" % a) for a in range(PASSES)]
         v2 = held([P, S2], U32, "v2")
+        v2_sc_rows = held([P, S2], U8, "v2_sc_rows")
         v2_sc = held([P, S2], U8, "v2_sc")
         cs_sb = held([P, PACK], F32, "cs_sb")
         fl_sb = held([P, M_TILES], F32, "fl_sb")
@@ -70,79 +73,72 @@ def tile_list_chop_seeding_page_kernel(
         wgo_sb = held([P, S], F32, "wgo_sb")
         page = [held([P, T2], F32, "page%d" % m) for m in range(M_TILES)]
 
-        ident = held([P, P], F32, "ident")
-        make_identity(nc, ident[:])
-
         nc.vector.memset(w_sc_raw[:].bitcast(I32), 0)
         nc.vector.memset(tab_sc[32:64, :].bitcast(I32), 0)
         nc.vector.memset(tab_sc[64:128, :].bitcast(I32), 0)
         for a in range(PASSES):
             nc.vector.memset(v_sc[a][:].bitcast(I32), 0)
         nc.gpsimd.memset(tab2_sc[:].bitcast(I32), 0)
+        nc.gpsimd.memset(v2_sc[:].bitcast(I32), 0)
+        ident = held([P, P], F32, "ident")
+        make_identity(nc, ident[:])
 
-        def load_weight_scales(row0, scales, q):
-            r = 32 * q + row0
+        def load_weight_scales(row0, scales, r):
             nc.sync.dma_start(
-                w_sc_raw[r : r + 4, :].bitcast(I32).rearrange("p (a c) -> p a c", a=PASSES),
-                scales[:, 4 * q : 4 * q + 4, :].rearrange("a r c -> r a c").bitcast(I32),
+                w_sc_raw[row0 + r : P : 32, :].bitcast(I32).rearrange("p (a c) -> p a c", a=PASSES),
+                scales[:, r : 16 : 4, :].rearrange("a q c -> q a c").bitcast(I32),
             )
 
         def load_table_half(a, u):
             cols = slice(u * T // 2, (u + 1) * T // 2)
             nc.sync.dma_start(tab[a][:, cols], tab_words[a].rearrange("p t i -> p (t i)").bitcast(I32)[:, cols])
 
-        def move_plane(a, q):
-            r = 16 * a + 4 * q
-            nc.sync.dma_start(v_sc[a][32 * q : 32 * q + 4, :].bitcast(I32), v_sc_rows[r : r + 4, :].bitcast(I32))
+        def move_rows(plane, rows, row0, r):
+            nc.sync.dma_start(plane[r:P:32, :].bitcast(I32), rows[row0 + r : row0 + 16 : 4, :].bitcast(I32))
 
         def load_w2(a):
             nc.sync.dma_start(
                 w2_raw[a][:], w2[512 * a : 512 * (a + 1), :].rearrange("(p j) c -> p (j c)", j=PACK)
             )
 
+        def load_w3():
+            nc.sync.dma_start(
+                w3_raw[:].rearrange("p (a c) -> p a c", a=PASSES),
+                w3_words.rearrange("a p c i -> p a (c i)").bitcast(I32),
+            )
+
+        def load_w1():
+            nc.sync.dma_start(
+                w1_raw[:].bitcast(I32).rearrange("p (a c) -> p a c", a=PASSES),
+                w1_words.rearrange("a p c -> p a c").bitcast(I32),
+            )
+
+        def load_tab2_scales():
+            nc.sync.dma_start(tab2_sc[0:16, :].bitcast(I32), tab2_scales[0].bitcast(I32))
+
+        def load_cs():
+            nc.sync.dma_start(cs_sb[:], cs.rearrange("(p t) -> p t", t=PACK))
+
+        small = [load_w1, load_tab2_scales]
+        small += [partial(load_weight_scales, 4, w3_scales, r) for r in range(4)]
+        small += [partial(load_weight_scales, 0, w1_scales, r) for r in range(4)]
+        small += [partial(move_rows, v_sc[a], v_sc_rows, 16 * a, r) for a in range(PASSES) for r in range(4)]
+        small += [load_cs]
+        large = [load_w3, partial(load_table_half, 1, 0), partial(load_table_half, 1, 1), partial(load_w2, 0)]
+
         nc.sync.dma_start(tab_sc[0:32, :].bitcast(I32), tab_scales.rearrange("a q t -> (a q) t").bitcast(I32))
         nc.sync.dma_start(idx[:], offs)
         load_table_half(0, 0)
         nc.sync.dma_start(idx2[:], offs2)
         nc.sync.dma_start(idx3[:], offs3)
-        nc.sync.dma_start(cs_sb[:], cs.rearrange("(p t) -> p t", t=PACK))
         load_table_half(0, 1)
-        nc.sync.dma_start(
-            w3_raw[:].rearrange("p (a c) -> p a c", a=PASSES),
-            w3_words.rearrange("a p c i -> p a (c i)").bitcast(I32),
-        )
-        load_weight_scales(4, w3_scales, 0)
-        load_weight_scales(4, w3_scales, 1)
-        nc.sync.dma_start(
-            w1_raw[:].bitcast(I32).rearrange("p (a c) -> p a c", a=PASSES),
-            w1_words.rearrange("a p c -> p a c").bitcast(I32),
-        )
-        load_weight_scales(4, w3_scales, 2)
-        load_weight_scales(4, w3_scales, 3)
-        load_table_half(1, 0)
-        for q in range(QUADS):
-            load_weight_scales(0, w1_scales, q)
         nc.vector.tensor_copy(v_sc_rows[:], tab_sc[:].indirect(idx[:]))
-        moves = [(a, q) for a in range(PASSES) for q in range(QUADS)]
-        for a, q in moves[:2]:
-            move_plane(a, q)
-        load_table_half(1, 1)
-        for a, q in moves[2:]:
-            move_plane(a, q)
-        load_w2(0)
-        for q in range(QUADS):
-            nc.sync.dma_start(
-                tab2_sc[32 * q : 32 * q + 4, :].bitcast(I32),
-                tab2_scales[0, 4 * q : 4 * q + 4, :].bitcast(I32),
-            )
+        for n, load in enumerate(large):
+            load()
+            for dma in small[SMALL_RUN * n : SMALL_RUN * (n + 1)]:
+                dma()
         load_w2(1)
         nc.sync.dma_start(tab2[:], tab2_words[0].rearrange("p t i -> p (t i)").bitcast(I32))
-        with nc.allow_non_contiguous_dma(reason="one value to a partition"):
-            nc.sync.dma_start(fl_sb[:], fl.rearrange("(m p) -> p m", p=P))
-            nc.sync.dma_start(av_sb[:], av.rearrange("(m p) -> p m", p=P))
-        nc.sync.dma_start(wgo_sb[:], wgo)
-        for m in range(M_TILES):
-            nc.sync.dma_start(page[m][:], page1[P * m : P * (m + 1), :])
 
         def gather_table(a):
             for u in range(S // HALF):
@@ -150,6 +146,15 @@ def tile_list_chop_seeding_page_kernel(
                 nc.vector.tensor_copy(v[a][u][:], tab[a][:].bitcast(U32).indirect(idx[:, cols]))
 
         gather_table(0)
+        nc.vector.tensor_copy(v2_sc_rows[:], tab2_sc[:].indirect(idx2[:]))
+        for r in range(4):
+            move_rows(v2_sc, v2_sc_rows, 0, r)
+        with nc.allow_non_contiguous_dma(reason="one value to a partition"):
+            nc.sync.dma_start(fl_sb[:], fl.rearrange("(m p) -> p m", p=P))
+            nc.sync.dma_start(av_sb[:], av.rearrange("(m p) -> p m", p=P))
+        nc.sync.dma_start(wgo_sb[:], wgo)
+        for m in range(M_TILES):
+            nc.sync.dma_start(page[m][:], page1[P * m : P * (m + 1), :])
 
         nc.vector.tensor_copy(
             w3[:].rearrange("p (a t q) -> p a q t", a=PASSES, t=PACK),
@@ -178,7 +183,6 @@ def tile_list_chop_seeding_page_kernel(
                     in_=w2_bf[a][:, 1024 * u : 1024 * (u + 1)],
                 )
 
-        nc.vector.tensor_copy(v2_sc[:], tab2_sc[:].indirect(idx2[:]))
         nc.vector.tensor_copy(v2[:], tab2[:].bitcast(U32).indirect(idx2[:]))
 
         def moving(a, tok):

from contextlib import ExitStack
from functools import partial

import concourse.mybir as mybir
from concourse.masks import make_identity

K, H, T, S, T2, T3, S2 = 1024, 512, 4096, 1024, 2048, 2048, 512
FLOPS = 2 * 3 * K * H * S + 2 * H * S2 * S

F32 = mybir.dt.float32
BF16 = mybir.dt.bfloat16
I32 = mybir.dt.int32
U32 = mybir.dt.uint32
U16 = mybir.dt.uint16
U8 = mybir.dt.uint8
FP8X4 = mybir.dt.float8_e4m3fn_x4
FP4X4 = mybir.dt.float4_e2m1fn_x4
MULT = mybir.AluOpType.mult
ADD = mybir.AluOpType.add
MAX = mybir.AluOpType.max
COPY = mybir.ActivationFunctionType.Copy

P = 128
PACK = 4
PASSES = K // (P * PACK)
QUADS = 4
HALF = 512
BANK = 512
M_TILES = S2 // P
CAST_SPLIT = (88, 48)
SMALL_RUN = 6


def tile_list_chop_seeding_page_kernel(
    tc, tab_words, tab_scales, tab2_words, tab2_scales, w1_words, w1_scales, w2,
    w3_words, w3_scales, cs, fl, av, page1, wgo, offs, offs2, offs3, out,
):
    nc = tc.nc
    with ExitStack() as ctx:
        keep = ctx.enter_context(tc.tile_pool(name="keep", bufs=1))
        ring = ctx.enter_context(tc.tile_pool(name="ring", bufs=2))
        psum = ctx.enter_context(tc.psum_pool(name="psum", bufs=2))

        def held(shape, dtype, name):
            return keep.tile(shape, dtype, name=name, align_bytes=64)

        idx = held([P, S // 16], U16, "idx")
        idx2 = held([P, S2 // 16], U16, "idx2")
        idx3 = held([P, S // 16], U16, "idx3")
        tab = [held([P, T], I32, "tab%d" % a) for a in range(PASSES)]
        tab_sc = held([P, T], U8, "tab_sc")
        tab2 = held([P, T3], I32, "tab2")
        tab2_sc = held([P, T3], U8, "tab2_sc")
        w_sc_raw = held([P, PASSES * H], U8, "w_sc_raw")
        w_sc = held([P, PASSES * H], U8, "w_sc")
        w1_raw = held([P, PASSES * H * 2], U8, "w1_raw")
        w1 = held([P, PASSES * H * 2], U8, "w1")
        w3_raw = held([P, PASSES * H], I32, "w3_raw")
        w3 = held([P, PASSES * H], I32, "w3")
        w2_raw = [held([P, PACK * H], F32, "w2_raw%d" % a) for a in range(PASSES)]
        w2_bf = [held([P, PACK * H], BF16, "w2_bf%d" % a) for a in range(PASSES)]
        w2_q = [held([P, H], U32, "w2_q%d" % a) for a in range(PASSES)]
        w2_sc = [held([P, H], U8, "w2_sc%d" % a) for a in range(PASSES)]
        v = [[held([P, HALF], U32, "v%d_%d" % (a, u)) for u in range(S // HALF)] for a in range(PASSES)]
        v_sc_rows = held([P, S], U8, "v_sc_rows")
        v_sc = [held([P, S], U8, "v_sc%d" % a) for a in range(PASSES)]
        v2 = held([P, S2], U32, "v2")
        v2_sc_rows = held([P, S2], U8, "v2_sc_rows")
        v2_sc = held([P, S2], U8, "v2_sc")
        cs_sb = held([P, PACK], F32, "cs_sb")
        fl_sb = held([P, M_TILES], F32, "fl_sb")
        av_sb = held([P, M_TILES], F32, "av_sb")
        wgo_sb = held([P, S], F32, "wgo_sb")
        page = [held([P, T2], F32, "page%d" % m) for m in range(M_TILES)]

        nc.vector.memset(w_sc_raw[:].bitcast(I32), 0)
        nc.vector.memset(tab_sc[32:64, :].bitcast(I32), 0)
        nc.vector.memset(tab_sc[64:128, :].bitcast(I32), 0)
        for a in range(PASSES):
            nc.vector.memset(v_sc[a][:].bitcast(I32), 0)
        nc.gpsimd.memset(tab2_sc[:].bitcast(I32), 0)
        nc.gpsimd.memset(v2_sc[:].bitcast(I32), 0)
        ident = held([P, P], F32, "ident")
        make_identity(nc, ident[:])

        def load_weight_scales(row0, scales, r):
            nc.sync.dma_start(
                w_sc_raw[row0 + r : P : 32, :].bitcast(I32).rearrange("p (a c) -> p a c", a=PASSES),
                scales[:, r : 16 : 4, :].rearrange("a q c -> q a c").bitcast(I32),
            )

        def load_table_half(a, u):
            cols = slice(u * T // 2, (u + 1) * T // 2)
            nc.sync.dma_start(tab[a][:, cols], tab_words[a].rearrange("p t i -> p (t i)").bitcast(I32)[:, cols])

        def move_rows(plane, rows, row0, r):
            nc.sync.dma_start(plane[r:P:32, :].bitcast(I32), rows[row0 + r : row0 + 16 : 4, :].bitcast(I32))

        def load_w2(a):
            nc.sync.dma_start(
                w2_raw[a][:], w2[512 * a : 512 * (a + 1), :].rearrange("(p j) c -> p (j c)", j=PACK)
            )

        def load_w3():
            nc.sync.dma_start(
                w3_raw[:].rearrange("p (a c) -> p a c", a=PASSES),
                w3_words.rearrange("a p c i -> p a (c i)").bitcast(I32),
            )

        def load_w1():
            nc.sync.dma_start(
                w1_raw[:].bitcast(I32).rearrange("p (a c) -> p a c", a=PASSES),
                w1_words.rearrange("a p c -> p a c").bitcast(I32),
            )

        def load_tab2_scales():
            nc.sync.dma_start(tab2_sc[0:16, :].bitcast(I32), tab2_scales[0].bitcast(I32))

        def load_cs():
            nc.sync.dma_start(cs_sb[:], cs.rearrange("(p t) -> p t", t=PACK))

        small = [load_w1, load_tab2_scales]
        small += [partial(load_weight_scales, 4, w3_scales, r) for r in range(4)]
        small += [partial(load_weight_scales, 0, w1_scales, r) for r in range(4)]
        small += [partial(move_rows, v_sc[a], v_sc_rows, 16 * a, r) for a in range(PASSES) for r in range(4)]
        small += [load_cs]
        large = [load_w3, partial(load_table_half, 1, 0), partial(load_table_half, 1, 1), partial(load_w2, 0)]

        nc.sync.dma_start(tab_sc[0:32, :].bitcast(I32), tab_scales.rearrange("a q t -> (a q) t").bitcast(I32))
        nc.sync.dma_start(idx[:], offs)
        load_table_half(0, 0)
        nc.sync.dma_start(idx2[:], offs2)
        nc.sync.dma_start(idx3[:], offs3)
        load_table_half(0, 1)
        nc.vector.tensor_copy(v_sc_rows[:], tab_sc[:].indirect(idx[:]))
        for n, load in enumerate(large):
            load()
            for dma in small[SMALL_RUN * n : SMALL_RUN * (n + 1)]:
                dma()
        load_w2(1)
        nc.sync.dma_start(tab2[:], tab2_words[0].rearrange("p t i -> p (t i)").bitcast(I32))

        def gather_table(a):
            for u in range(S // HALF):
                cols = slice(u * HALF // 16, (u + 1) * HALF // 16)
                nc.vector.tensor_copy(v[a][u][:], tab[a][:].bitcast(U32).indirect(idx[:, cols]))

        gather_table(0)
        nc.vector.tensor_copy(v2_sc_rows[:], tab2_sc[:].indirect(idx2[:]))
        for r in range(4):
            move_rows(v2_sc, v2_sc_rows, 0, r)
        with nc.allow_non_contiguous_dma(reason="one value to a partition"):
            nc.sync.dma_start(fl_sb[:], fl.rearrange("(m p) -> p m", p=P))
            nc.sync.dma_start(av_sb[:], av.rearrange("(m p) -> p m", p=P))
        nc.sync.dma_start(wgo_sb[:], wgo)
        for m in range(M_TILES):
            nc.sync.dma_start(page[m][:], page1[P * m : P * (m + 1), :])

        nc.vector.tensor_copy(
            w3[:].rearrange("p (a t q) -> p a q t", a=PASSES, t=PACK),
            w3_raw[:].rearrange("p (a q t) -> p a q t", a=PASSES, t=PACK),
        )
        nc.vector.tensor_copy(
            w1[:].bitcast(U16).rearrange("p (a t q) -> p a q t", a=PASSES, t=PACK),
            w1_raw[:].bitcast(U16).rearrange("p (a q t) -> p a q t", a=PASSES, t=PACK),
        )
        nc.vector.tensor_copy(
            w_sc[:].rearrange("p (a t q) -> p a q t", a=PASSES, t=PACK),
            w_sc_raw[:].rearrange("p (a q t) -> p a q t", a=PASSES, t=PACK),
        )
        gather_table(1)
        for a in range(PASSES):
            dst = w2_bf[a][:].rearrange("p (t q j) -> p q j t", t=PACK, j=PACK)
            src = w2_raw[a][:].rearrange("p (j q t) -> p q j t", t=PACK, j=PACK)
            for u in range(2):
                split, ts = CAST_SPLIT[u], slice(2 * u, 2 * u + 2)
                nc.scalar.copy(dst[:, split:, :, ts], src[:, split:, :, ts])
                nc.vector.tensor_copy(dst[:, :split, :, ts], src[:, :split, :, ts])
            for u in range(2):
                nc.vector.quantize_mx(
                    out=w2_q[a][:, 256 * u : 256 * (u + 1)].bitcast(FP8X4),
                    scales=w2_sc[a][:, 256 * u : 256 * (u + 1)],
                    in_=w2_bf[a][:, 1024 * u : 1024 * (u + 1)],
                )

        nc.vector.tensor_copy(v2[:], tab2[:].bitcast(U32).indirect(idx2[:]))

        def moving(a, tok):
            u, o = divmod(tok.start, HALF)
            return v[a][u][:, o : o + tok.stop - tok.start].bitcast(FP8X4)

        def products(tok, t0, per_bank):
            width = tok.stop - tok.start
            c1 = psum.tile([P, per_bank, width], F32, name="c1")
            c2 = psum.tile([P, per_bank, width], F32, name="c2")
            c3 = psum.tile([P, per_bank, width], F32, name="c3")
            for i in range(per_bank):
                t = t0 + i
                for a in range(PASSES):
                    w = slice(a * H + t * P, a * H + (t + 1) * P)
                    nc.tensor.matmul_mx(
                        out=c3[:, i, :], lhsT=w3[:, w].bitcast(FP8X4), lhsT_scale=w_sc[4:P, w],
                        rhs=moving(a, tok), rhs_scale=v_sc[a][:, tok],
                        start=(a == 0), stop=(a == PASSES - 1),
                    )
            for a in range(PASSES):
                for i in range(per_bank):
                    t = t0 + i
                    w = slice(t * P, (t + 1) * P)
                    nc.tensor.matmul_mx(
                        out=c2[:, i, :], lhsT=w2_q[a][:, w].bitcast(FP8X4), lhsT_scale=w2_sc[a][:, w],
                        rhs=moving(a, tok), rhs_scale=v_sc[a][:, tok],
                        start=(a == 0 and i == 0), stop=(a == PASSES - 1 and i == per_bank - 1),
                    )
            for i in range(per_bank):
                t = t0 + i
                for a in range(PASSES):
                    w0 = a * H + t * P
                    nc.tensor.matmul_mx(
                        out=c1[:, i, :], lhsT=w1[:, 2 * w0 : 2 * (w0 + P)].bitcast(FP4X4),
                        lhsT_scale=w_sc[:, w0 : w0 + P],
                        rhs=moving(a, tok), rhs_scale=v_sc[a][:, tok],
                        start=(a == 0), stop=(a == PASSES - 1),
                    )
            return c1, c2, c3

        def quantise_h(h_bf, width):
            h_q = ring.tile([P, width], U32, name="h_q", align_bytes=64)
            h_sc = ring.tile([P, width], U8, name="h_sc", align_bytes=64)
            nc.vector.quantize_mx(out=h_q[:].bitcast(FP8X4), scales=h_sc[:], in_=h_bf[:])
            return h_q, h_sc

        def features(tok):
            width = tok.stop - tok.start
            per_bank = BANK // width
            h_planes = ring.tile([P, PACK, width], BF16, name="h_planes", align_bytes=64)
            banks = []
            for t0 in range(0, PACK, per_bank):
                c1, c2, c3 = products(tok, t0, per_bank)
                c3_sb = ring.tile([P, per_bank, width], F32, name="c3_sb")
                nc.scalar.copy(c3_sb[:], c3[:])
                larger = ring.tile([P, per_bank, width], F32, name="larger")
                nc.vector.tensor_tensor(larger[:], c2[:], c3_sb[:], MAX)
                banks.append((t0, c1, larger))
            for t0, c1, larger in banks:
                for i in range(per_bank):
                    t = t0 + i
                    nc.vector.scalar_tensor_tensor(
                        h_planes[:, t, :], c1[:, i, :], cs_sb[:, t : t + 1], larger[:, i, :], MULT, ADD
                    )
            h_bf = ring.tile([P, width * PACK], BF16, name="h_bf", align_bytes=64)
            nc.scalar.copy(
                h_bf[:].rearrange("p (c i t) -> p c t i", i=4, t=PACK),
                h_planes[:].rearrange("p t (c i) -> p c t i", i=4),
            )
            return quantise_h(h_bf, width)

        def features_added_in_psum(tok):
            blocks = BANK // P
            terms = []
            for t in range(PACK):
                c1, c2, c3 = products(tok, t, 1)
                if t == PACK - 1:
                    c3_sb = keep.tile([P, BANK], F32, name="c3_last", tag="hold_a", align_bytes=64)
                else:
                    c3_sb = ring.tile([P, BANK], F32, name="c3_sb")
                nc.scalar.copy(c3_sb[:], c3[:, 0, :])
                scaled = held([P, BANK], F32, "scaled%d" % t)
                nc.scalar.activation(scaled[:], c1[:, 0, :], COPY, scale=cs_sb[:, t : t + 1])
                larger = held([P, BANK], F32, "larger%d" % t)
                nc.vector.tensor_tensor(larger[:], c2[:, 0, :], c3_sb[:], MAX)
                terms.append((scaled, larger))
            h_bf = keep.tile([P, BANK * PACK], BF16, name="h_bf_last", tag="hold_b", align_bytes=64)
            sums = [psum.tile([P, PACK, P], F32, name="h_t", tag=tag) for tag in ("e", "e", "c1", "c3")]
            for t in range(PACK):
                for b in range(blocks):
                    for n, term in enumerate(terms[t]):
                        nc.tensor.matmul(
                            sums[b][:, t, :], term[:, b * P : (b + 1) * P], ident[:],
                            start=(n == 0), stop=(n == 1), is_transpose=True,
                        )
            for b0 in range(0, blocks, 2):
                words = psum.tile([P, 2, 2, P], F32, name="words", tag="c2")
                for i in range(2):
                    h_t = ring.tile([P, 2 * P * 2], BF16, name="h_t_bf", bufs=4, align_bytes=64)
                    nc.scalar.copy(
                        h_t[:].rearrange("p (u q e) -> p u q e", u=2, e=2),
                        sums[b0 + i][:].rearrange("p (u e) q -> p u q e", u=2),
                    )
                    for u in range(2):
                        nc.tensor.transpose(words[:, i, u, :], h_t[:].bitcast(F32)[:, u * P : (u + 1) * P], ident[:])
                nc.scalar.copy(
                    h_bf[:].bitcast(F32)[:, b0 * 2 * P : (b0 + 2) * 2 * P].rearrange("p (b n u) -> p b n u", b=2, u=2),
                    words[:].rearrange("p b u n -> p b n u"),
                )
            return quantise_h(h_bf, BANK)

        def scores(tok, h_q, h_sc):
            width = tok.stop - tok.start
            per_bank = BANK // width
            rows = []
            for m0 in range(0, M_TILES, per_bank):
                e = psum.tile([P, per_bank, width], F32, name="e")
                for i in range(per_bank):
                    m = m0 + i
                    nc.tensor.matmul_mx(
                        out=e[:, i, :], lhsT=v2[:, m * P : (m + 1) * P].bitcast(FP8X4),
                        lhsT_scale=v2_sc[:, m * P : (m + 1) * P],
                        rhs=h_q[:].bitcast(FP8X4), rhs_scale=h_sc[:], start=True, stop=True,
                    )
                e_sb = ring.tile([P, per_bank, width], F32, name="e_sb", bufs=4)
                nc.scalar.copy(e_sb[:], e[:])
                rows.extend([e_sb[:, i, :] for i in range(per_bank)])
            return rows

        def place(tok, e_rows, groups, last):
            width = tok.stop - tok.start
            cols = slice(tok.start // 16, tok.stop // 16)
            for tag, ms in groups:
                y = keep.tile([P, len(ms), width], F32, name="y", tag=tag, align_bytes=64)
                for i, m in enumerate(ms):
                    nc.vector.tensor_scalar(
                        y[:, i, :], e_rows[m], fl_sb[:, m : m + 1], av_sb[:, m : m + 1], MAX, MULT
                    )
                for i, m in enumerate(ms):
                    nc.vector.tensor_tensor(page[m][:].indirect(idx3[:, cols]), y[:, i, :], wgo_sb[:, tok], MULT)
                    if last:
                        nc.sync.dma_start(out[P * m : P * (m + 1), :], page[m][:])

        first, second, third = slice(0, 256), slice(256, 512), slice(512, 1024)
        h0 = features(first)
        h1 = features(second)
        place(first, scores(first, *h0), (("y0a", (0, 1)), ("y0b", (2, 3))), False)
        e1 = scores(second, *h1)
        h2 = features_added_in_psum(third)
        place(second, e1, (("hold_a", (0, 1)), ("hold_b", (2, 3))), False)
        place(third, scores(third, *h2), (("y2a", (0,)), ("y2b", (1,)), ("y2c", (2,)), ("y2d", (3,))), True)
